import numpy as np
import ml_dtypes


def mxq(x, axis, fmt="e4m3"):
    dtype, down = {"e4m3": (ml_dtypes.float8_e4m3fn, 7), "e5m2": (ml_dtypes.float8_e5m2, 14)}[fmt]
    v = np.moveaxis(np.asarray(x, np.float32).astype(ml_dtypes.bfloat16).astype(np.float64), axis, -1)
    blocks = v.reshape(v.shape[:-1] + (-1, 32))
    amax = np.abs(blocks).max(-1, keepdims=True)
    byte = np.maximum(np.where(amax > 0, np.frexp(amax)[1] - 1 + 127, 0) - down, 1)
    scale = np.exp2(byte - 127.0)
    codes = (blocks / scale).astype(np.float32).astype(dtype).astype(np.float64)
    return np.moveaxis((codes * scale).reshape(v.shape), -1, axis)


WIDE = False


def mx_kscale(k):
    if not WIDE:
        return np.ones(k)
    levels = np.array([10, -10, 5, -5, 0])
    if k % 512:
        return np.exp2(np.random.permutation(np.resize(levels, k // 32))).repeat(32)
    a = np.empty((k // 512, 16))
    for p in range(k // 512):
        a[p, :8] = np.random.permutation(np.resize(levels, 8))
        for g in range(8):
            far = levels[np.abs(levels - a[p, g]) >= 10]
            a[p, g + 8] = far[np.random.randint(len(far))]
    return np.exp2(a.ravel()).repeat(32)


def f64(x):
    return np.asarray(x).astype(np.float64)


def striped(idx):
    return np.tile(np.asarray(idx).reshape(-1, 16).T, (8, 1)).astype(np.uint16)


def unstriped(offs):
    return offs[:16].T.reshape(-1).astype(np.int64)


E2M1 = np.array([0.0, 0.5, 1.0, 1.5, 2.0, 3.0, 4.0, 6.0, -0.0, -0.5, -1.0, -1.5, -2.0, -3.0, -4.0, -6.0])


def pack_weight(w, fmt):
    k, n = w.shape
    w = f64(np.asarray(w, np.float32).astype(ml_dtypes.bfloat16)).reshape(k // 32, 32, n)
    amax = np.abs(w).max(1)
    if fmt == "e4m3":
        byte = np.frexp(amax)[1] - 1 + 127 - 7
    else:
        mant, ex = np.frexp(amax / 6.0)
        byte = np.where(mant > 0.5, ex, ex - 1) + 127
    byte = np.clip(np.where(amax > 0, byte, 1), 1, 254)
    scaled = (w * np.exp2(127.0 - byte)[:, None, :]).reshape(k, n).astype(np.float32)
    by_word = np.ascontiguousarray(scaled.reshape(k // 512, 128, 4, n).transpose(0, 1, 3, 2))
    if fmt == "e4m3":
        words = by_word.astype(ml_dtypes.float8_e4m3fn).view(np.uint8)
    else:
        c = by_word.astype(ml_dtypes.float4_e2m1fn).view(np.uint8) & 0xF
        words = (c[..., 0::2] | (c[..., 1::2] << 4)).reshape(k // 512, 128, 2 * n)
    return np.ascontiguousarray(words), np.ascontiguousarray(byte.astype(np.uint8).reshape(k // 512, 16, n))


def unpack_weight(words, scales, fmt):
    g, _, n = scales.shape
    words = np.ascontiguousarray(words).reshape(g, 128, n, -1)
    if fmt == "e4m3":
        vals = words.view(ml_dtypes.float8_e4m3fn).astype(np.float64)
    else:
        nib = np.empty((g, 128, n, 4), np.uint8)
        nib[..., 0::2] = words & 0xF
        nib[..., 1::2] = words >> 4
        vals = E2M1[nib]
    vals = vals * np.repeat(np.exp2(scales.astype(np.float64) - 127.0), 8, axis=1)[..., None]
    return vals.transpose(0, 1, 3, 2).reshape(g * 512, n)


B, N, T, D, DV, NQ = 1, 512, 2048, 512, 256, 256


def setup_inputs():
    n = np.random.standard_normal
    idx = np.sort(np.random.permutation(T)[:B * N].reshape(B, N), axis=1).reshape(-1)
    s = mx_kscale(D)[:, None]
    u = np.ones(T)
    u[idx] = mx_kscale(B * N)
    r = np.random.uniform(0.5, 2.0, T)
    k = n((D, T)) / s
    v = n((DV, T)) / (u * r)
    kp = pack_weight(k, "e4m3")
    return {
        "qT": (n((B, D, NQ)) * s * (0.60 / np.sqrt(D))).astype(np.float32),
        "k_words": kp[0],
        "k_scales": kp[1],
        "vT": v.astype(np.float32),
        "vs": np.tile(u * r, (128, 1)).astype(np.float32),
        "kb": np.tile(n(T), (128, 1)).astype(np.float32),
        "og": n((B, NQ, DV)).astype(np.float32),
        "offs": striped(idx),
    }


def reference(qT, k_words, k_scales, vT, vs, kb, og, offs):
    idx = unstriped(offs)
    k = unpack_weight(k_words, k_scales, "e4m3")
    v = f64(vT)
    pick = lambda x: x[:, idx].reshape(x.shape[0], B, N).transpose(1, 0, 2)
    q = f64(qT)
    score = mxq(q, 1, "e4m3").transpose(0, 2, 1) @ pick(k)
    score = score + pick(f64(kb))[:, :1, :]
    p = score / (1.0 + np.exp(-score))
    w = p * pick(f64(vs))[:, :1, :]
    y = mxq(w, 2, "e4m3") @ mxq(pick(v).transpose(0, 2, 1), 1, "e4m3")
    y = y / 16.0
    y = y / (1.0 + np.exp(-f64(og)))
    return y

@@ -1,0 +1,184 @@
+from contextlib import ExitStack
+
+import concourse.mybir as mybir
+
+F32 = mybir.dt.float32
+BF16 = mybir.dt.bfloat16
+I32 = mybir.dt.int32
+U32 = mybir.dt.uint32
+U16 = mybir.dt.uint16
+U8 = mybir.dt.uint8
+FP8X4 = mybir.dt.float8_e4m3fn_x4
+ACT = mybir.ActivationFunctionType
+MULT = mybir.AluOpType.mult
+
+P = 128
+T, N, D, DV, NQ = 2048, 512, 512, 256, 256
+FLOPS = 2 * NQ * N * (D + DV)
+
+
+def tile_attend_silu_gate_bias_srt_kernel(tc, qT, k_words, k_scales, vT, vs, kb, og, offs, out):
+    nc = tc.nc
+    with ExitStack() as ctx:
+        sb = ctx.enter_context(tc.tile_pool(name="sb", bufs=1))
+        late = ctx.enter_context(tc.tile_pool(name="late", bufs=1))
+        ps = ctx.enter_context(tc.psum_pool(name="ps", bufs=1))
+
+        offsets = sb.tile([P, N // 16], U16, name="offsets")
+        nc.sync.dma_start(offsets[:], offs)
+
+        ks_pool = sb.tile([P, T], U8, name="ks_pool", align_bytes=64)
+        kb_pool = sb.tile([P, T], F32, name="kb_pool", align_bytes=64)
+        vs_pool = sb.tile([P, T], F32, name="vs_pool", align_bytes=64)
+        nc.vector.memset(ks_pool[:].bitcast(I32), 0)
+        nc.vector.memset(kb_pool[0 : P - 1, :], 0.0)
+        nc.vector.memset(vs_pool[0 : P - 1, :], 0.0)
+        nc.sync.dma_start(kb_pool[P - 1 : P, :], kb[0:1, :])
+        nc.sync.dma_start(vs_pool[P - 1 : P, :], vs[0:1, :])
+
+        og_sb = sb.tile([P, 2, DV], F32, name="og_sb")
+        nc.sync.dma_start(og_sb[:], og[0].rearrange("(h p) e -> p h e", p=P))
+        kw_pool = sb.tile([P, T], I32, name="kw_pool", align_bytes=64)
+        nc.sync.dma_start(kw_pool[:], k_words[0].rearrange("p n t -> p (n t)").bitcast(I32))
+        for quad in range(4):
+            nc.sync.dma_start(
+                ks_pool[32 * quad : 32 * quad + 4, :].bitcast(I32),
+                k_scales[0, 4 * quad : 4 * quad + 4, :].bitcast(I32),
+            )
+
+        q_bytes = 4 * NQ * 4
+        blank = late.tile([P, P], F32, name="blank", offset=q_bytes - 256)
+        ident = sb.tile([P, P], F32, name="ident")
+        nc.gpsimd.memset(blank[:], 0.0)
+        nc.gpsimd.affine_select(
+            out=ident[:],
+            in_=blank[:],
+            compare_op=mybir.AluOpType.not_equal,
+            fill=1.0,
+            base=0,
+            pattern=[[-1, P]],
+            channel_multiplier=1,
+        )
+        q_raw = late.tile([P, 4, NQ], F32, name="q_raw", offset=0)
+        nc.sync.dma_start(q_raw[:], qT[0].rearrange("(p j) q -> p j q", j=4))
+        v_pool = late.tile([P, 2 * T], F32, name="v_pool", offset=q_bytes)
+        for c in range(2):
+            nc.sync.dma_start(v_pool[:, c * T : (c + 1) * T], vT[c * P : (c + 1) * P, :])
+
+        gate = sb.tile([P, 2, DV], F32, name="gate")
+        nc.scalar.activation(gate[:], og_sb[:], ACT.Sigmoid)
+        warm = sb.tile([P, 1], F32, name="warm")
+        nc.scalar.activation(warm[:], gate[:, 0, 0:1], ACT.Silu)
+
+        q_bf = sb.tile([P, NQ, 4], BF16, name="q_bf", align_bytes=64)
+        nc.scalar.copy(
+            q_bf[:].rearrange("p (c i) t -> p c t i", i=2),
+            q_raw[:].rearrange("p t (c i) -> p c t i", i=2),
+        )
+
+        def dealt(tile):
+            return tile[:].bitcast(U32).rearrange("p (t g i) -> p g t i", t=4, i=4)
+
+        ks_got = sb.tile([P, N], U8, name="ks_got", tag="ks_vs", align_bytes=64)
+        nc.vector.tensor_copy(ks_got[:], ks_pool[:].indirect(offsets[:]))
+        k_codes = sb.tile([P, N], U32, name="k_codes", align_bytes=64)
+        nc.vector.tensor_copy(dealt(k_codes), kw_pool[:].bitcast(U32).indirect(offsets[:]))
+        k_plane = sb.tile([P, N], U8, name="k_plane", align_bytes=64)
+        nc.vector.tensor_copy(
+            k_plane[:].bitcast(I32).rearrange("p (t g) -> p t g", t=4),
+            ks_got[:].bitcast(I32).rearrange("p (g t) -> p t g", t=4),
+        )
+
+        def token_columns(pool, name, tag):
+            got = sb.tile([P, N], F32, name=name + "_got", tag=tag, align_bytes=64)
+            nc.vector.tensor_copy(dealt(got), pool[:].bitcast(U32).indirect(offsets[:]))
+            turned = ps.tile([P, 4, P], F32, name=name + "_turned")
+            for t in range(4):
+                nc.tensor.transpose(turned[:, t, :], got[:, t * P : (t + 1) * P], ident[:])
+            cols = sb.tile([P, 4], F32, name=name + "_cols")
+            nc.scalar.copy(cols[:], turned[:, :, P - 1])
+            return cols
+
+        kb_cols = token_columns(kb_pool, "kb", "kb_got")
+
+        q_codes = sb.tile([P, NQ], U32, name="q_codes", align_bytes=64)
+        q_plane = sb.tile([P, NQ], U8, name="q_plane", align_bytes=64)
+        nc.vector.quantize_mx(q_codes[:].bitcast(FP8X4), q_plane[:], q_bf[:].rearrange("p q t -> p (q t)"))
+
+        vs_cols = token_columns(vs_pool, "vs", "ks_vs")
+
+        silu = sb.tile([P, 4, NQ], F32, name="silu")
+        for pair in range(2):
+            scores = ps.tile([P, 2, NQ], F32, name="scores%d" % pair)
+            for u in range(2):
+                t = 2 * pair + u
+                nc.tensor.matmul_mx(
+                    scores[:, u, :],
+                    lhsT=k_codes[:, t * P : (t + 1) * P].bitcast(FP8X4),
+                    lhsT_scale=k_plane[:, t * P : (t + 1) * P],
+                    rhs=q_codes[:].bitcast(FP8X4),
+                    rhs_scale=q_plane[:],
+                    start=True,
+                    stop=True,
+                )
+            for u in range(2):
+                t = 2 * pair + u
+                nc.scalar.activation(silu[:, t, :], scores[:, u, :], ACT.Silu, bias=kb_cols[:, t : t + 1])
+
+        def values(c):
+            got = sb.tile([P, N], BF16, name="v_got%d" % c, align_bytes=64)
+            nc.vector.tensor_copy(
+                got[:].rearrange("p (u g i c) -> p g u c i", u=2, i=4, c=2),
+                v_pool[:, c * T : (c + 1) * T].indirect(offsets[:]),
+            )
+            turned = ps.tile([P, 2, P], F32, name="v_turned%d" % c)
+            words = got[:].bitcast(F32)
+            for u in range(2):
+                nc.tensor.transpose(turned[:, u, :], words[:, u * P : (u + 1) * P], ident[:])
+            v_bf = sb.tile([P, P * 4], BF16, name="v_bf%d" % c, align_bytes=64)
+            nc.scalar.copy(
+                v_bf[:].bitcast(F32).rearrange("p (e u) -> p e u", u=2),
+                turned[:].rearrange("p u e -> p e u"),
+            )
+            return v_bf
+
+        w_bf = sb.tile([P, NQ, 4], BF16, name="w_bf", align_bytes=64)
+
+        def weights(h):
+            rows = slice(h * P, (h + 1) * P)
+            nc.vector.tensor_tensor(
+                w_bf[:, rows, :].rearrange("p (c i) t -> p c t i", i=2),
+                silu[:, :, rows].rearrange("p t (c i) -> p c t i", i=2),
+                vs_cols[:].unsqueeze(1).unsqueeze(3).to_broadcast([P, P // 2, 4, 2]),
+                MULT,
+            )
+
+        v_bf0 = values(0)
+        weights(0)
+        v_bf1 = values(1)
+        weights(1)
+        w_codes = sb.tile([P, NQ], U32, name="w_codes", align_bytes=64)
+        w_plane = sb.tile([P, NQ], U8, name="w_plane", align_bytes=64)
+        nc.vector.quantize_mx(w_codes[:].bitcast(FP8X4), w_plane[:], w_bf[:].rearrange("p q t -> p (q t)"))
+
+        out_rows = out[0].rearrange("(h p) e -> p h e", p=P)
+        for c, v_bf in enumerate((v_bf0, v_bf1)):
+            v_codes = sb.tile([P, P], U32, name="v_codes%d" % c, align_bytes=64)
+            v_plane = sb.tile([P, P], U8, name="v_plane%d" % c, align_bytes=64)
+            nc.vector.quantize_mx(v_codes[:].bitcast(FP8X4), v_plane[:], v_bf[:])
+            y = ps.tile([P, 2, P], F32, name="y%d" % c)
+            for h in range(2):
+                nc.tensor.matmul_mx(
+                    y[:, h, :],
+                    lhsT=w_codes[:, h * P : (h + 1) * P].bitcast(FP8X4),
+                    lhsT_scale=w_plane[:, h * P : (h + 1) * P],
+                    rhs=v_codes[:].bitcast(FP8X4),
+                    rhs_scale=v_plane[:],
+                    start=True,
+                    stop=True,
+                )
+            result = sb.tile([P, 2, P], F32, name="result%d" % c)
+            nc.vector.scalar_tensor_tensor(
+                result[:], y[:], 1.0 / 16.0, gate[:, :, c * P : (c + 1) * P], MULT, MULT
+            )
+            nc.sync.dma_start(out_rows[:, :, c * P : (c + 1) * P], result[:])

@@ -27,50 +27,48 @@ def tile_attend_silu_gate_bias_srt_kernel(tc, qT, k_words, k_scales, vT, vs, kb,
         offsets = sb.tile([P, N // 16], U16, name="offsets")
         nc.sync.dma_start(offsets[:], offs)
 
+        row_bytes = T * 4
         ks_pool = sb.tile([P, T], U8, name="ks_pool", align_bytes=64)
-        kb_pool = sb.tile([P, T], F32, name="kb_pool", align_bytes=64)
-        vs_pool = sb.tile([P, T], F32, name="vs_pool", align_bytes=64)
-        nc.vector.memset(ks_pool[:].bitcast(I32), 0)
-        nc.vector.memset(kb_pool[0 : P - 1, :], 0.0)
-        nc.vector.memset(vs_pool[0 : P - 1, :], 0.0)
-        nc.sync.dma_start(kb_pool[P - 1 : P, :], kb[0:1, :])
-        nc.sync.dma_start(vs_pool[P - 1 : P, :], vs[0:1, :])
-
-        og_sb = sb.tile([P, 2, DV], F32, name="og_sb")
-        nc.sync.dma_start(og_sb[:], og[0].rearrange("(h p) e -> p h e", p=P))
-        kw_pool = sb.tile([P, T], I32, name="kw_pool", align_bytes=64)
-        nc.sync.dma_start(kw_pool[:], k_words[0].rearrange("p n t -> p (n t)").bitcast(I32))
-        for quad in range(4):
-            nc.sync.dma_start(
-                ks_pool[32 * quad : 32 * quad + 4, :].bitcast(I32),
-                k_scales[0, 4 * quad : 4 * quad + 4, :].bitcast(I32),
-            )
-
-        q_bytes = 4 * NQ * 4
-        blank = late.tile([P, P], F32, name="blank", offset=q_bytes - 256)
+        blank = late.tile([P, 2 * T + P], F32, name="blank", offset=row_bytes - 256, align_bytes=64)
+        nc.gpsimd.memset(blank[:, 0:P], 0.0)
+        nc.gpsimd.memset(ks_pool[:].bitcast(I32), 0)
         ident = sb.tile([P, P], F32, name="ident")
-        nc.gpsimd.memset(blank[:], 0.0)
         nc.gpsimd.affine_select(
             out=ident[:],
-            in_=blank[:],
+            in_=blank[:, 0:P],
             compare_op=mybir.AluOpType.not_equal,
             fill=1.0,
             base=0,
             pattern=[[-1, P]],
             channel_multiplier=1,
         )
-        q_raw = late.tile([P, 4, NQ], F32, name="q_raw", offset=0)
+        warm = sb.tile([P, 1], F32, name="warm", tag="warm_q", align_bytes=64)
+        nc.scalar.activation(warm[:], ident[:, 0:1], ACT.Silu)
+
+        kb_pool = late.tile([P, T], F32, name="kb_pool", offset=4 * row_bytes, align_bytes=64)
+        nc.vector.memset(kb_pool[0 : P - 1, 0:767], 0.0)
+        nc.vector.memset(kb_pool[0 : P - 1, 767:1536], 0.0)
+        nc.gpsimd.memset(kb_pool[0 : P - 1, 1536:T], 0.0)
+        nc.sync.dma_start(kb_pool[P - 1 : P, :], kb[0:1, :])
+        q_raw = sb.tile([P, 4, NQ], F32, name="q_raw")
         nc.sync.dma_start(q_raw[:], qT[0].rearrange("(p j) q -> p j q", j=4))
-        v_pool = late.tile([P, 2 * T], F32, name="v_pool", offset=q_bytes)
+        for quad in range(4):
+            nc.sync.dma_start(
+                ks_pool[32 * quad : 32 * quad + 4, :].bitcast(I32),
+                k_scales[0, 4 * quad : 4 * quad + 4, :].bitcast(I32),
+            )
+        kw_pool = late.tile([P, T], I32, name="kw_pool", offset=0, align_bytes=64)
+        nc.sync.dma_start(kw_pool[:], k_words[0].rearrange("p n t -> p (n t)").bitcast(I32))
+        vs_pool = late.tile([P, T], F32, name="vs_pool", offset=row_bytes, align_bytes=64)
+        nc.sync.dma_start(vs_pool[P - 1 : P, :], vs[0:1, :])
+        nc.gpsimd.memset(vs_pool[0 : P - 1, :], 0.0)
+        v_pool = []
         for c in range(2):
-            nc.sync.dma_start(v_pool[:, c * T : (c + 1) * T], vT[c * P : (c + 1) * P, :])
+            v_half = late.tile([P, T], F32, name="v_pool%d" % c, offset=(2 + c) * row_bytes, align_bytes=64)
+            nc.sync.dma_start(v_half[:], vT[c * P : (c + 1) * P, :])
+            v_pool.append(v_half)
 
-        gate = sb.tile([P, 2, DV], F32, name="gate")
-        nc.scalar.activation(gate[:], og_sb[:], ACT.Sigmoid)
-        warm = sb.tile([P, 1], F32, name="warm")
-        nc.scalar.activation(warm[:], gate[:, 0, 0:1], ACT.Silu)
-
-        q_bf = sb.tile([P, NQ, 4], BF16, name="q_bf", align_bytes=64)
+        q_bf = sb.tile([P, NQ, 4], BF16, name="q_bf", tag="warm_q", align_bytes=64)
         nc.scalar.copy(
             q_bf[:].rearrange("p (c i) t -> p c t i", i=2),
             q_raw[:].rearrange("p t (c i) -> p c t i", i=2),
@@ -79,106 +77,100 @@ def tile_attend_silu_gate_bias_srt_kernel(tc, qT, k_words, k_scales, vT, vs, kb,
         def dealt(tile):
             return tile[:].bitcast(U32).rearrange("p (t g i) -> p g t i", t=4, i=4)
 
-        ks_got = sb.tile([P, N], U8, name="ks_got", tag="ks_vs", align_bytes=64)
+        def token_columns(pool, got, name):
+            nc.vector.tensor_copy(dealt(got), pool[:].bitcast(U32).indirect(offsets[:]))
+            turned = ps.tile([P, 4, P], F32, name=name + "_turned", tag=name + "_bank")
+            for t in range(4):
+                nc.tensor.transpose(turned[:, t, :], got[:, t * P : (t + 1) * P], ident[:])
+            return turned[:, :, P - 1]
+
+        kb_got = sb.tile([P, N], F32, name="kb_got", tag="kb_og_v", align_bytes=64)
+        kb_cols = sb.tile([P, 4], F32, name="kb_cols", tag="kb_gate")
+        nc.scalar.copy(kb_cols[:], token_columns(kb_pool, kb_got, "kb"))
+        og_sb = sb.tile([P, 2, DV], F32, name="og_sb", tag="kb_og_v", align_bytes=64)
+        nc.sync.dma_start(og_sb[:], og[0].rearrange("(h p) e -> p h e", p=P))
+
+        ks_got = late.tile([P, N], U8, name="ks_got", offset=4 * row_bytes, align_bytes=64)
         nc.vector.tensor_copy(ks_got[:], ks_pool[:].indirect(offsets[:]))
-        k_codes = sb.tile([P, N], U32, name="k_codes", align_bytes=64)
-        nc.vector.tensor_copy(dealt(k_codes), kw_pool[:].bitcast(U32).indirect(offsets[:]))
         k_plane = sb.tile([P, N], U8, name="k_plane", align_bytes=64)
         nc.vector.tensor_copy(
             k_plane[:].bitcast(I32).rearrange("p (t g) -> p t g", t=4),
             ks_got[:].bitcast(I32).rearrange("p (g t) -> p t g", t=4),
         )
-
-        def token_columns(pool, name, tag):
-            got = sb.tile([P, N], F32, name=name + "_got", tag=tag, align_bytes=64)
-            nc.vector.tensor_copy(dealt(got), pool[:].bitcast(U32).indirect(offsets[:]))
-            turned = ps.tile([P, 4, P], F32, name=name + "_turned")
-            for t in range(4):
-                nc.tensor.transpose(turned[:, t, :], got[:, t * P : (t + 1) * P], ident[:])
-            cols = sb.tile([P, 4], F32, name=name + "_cols")
-            nc.scalar.copy(cols[:], turned[:, :, P - 1])
-            return cols
-
-        kb_cols = token_columns(kb_pool, "kb", "kb_got")
-
-        q_codes = sb.tile([P, NQ], U32, name="q_codes", align_bytes=64)
+        q_codes = late.tile([P, NQ], U32, name="q_codes", offset=4 * row_bytes + 1024, align_bytes=64)
         q_plane = sb.tile([P, NQ], U8, name="q_plane", align_bytes=64)
         nc.vector.quantize_mx(q_codes[:].bitcast(FP8X4), q_plane[:], q_bf[:].rearrange("p q t -> p (q t)"))
-
-        vs_cols = token_columns(vs_pool, "vs", "ks_vs")
+        k_codes = late.tile([P, N], U32, name="k_codes", offset=4 * row_bytes + 2048, align_bytes=64)
+        nc.vector.tensor_copy(dealt(k_codes), kw_pool[:].bitcast(U32).indirect(offsets[:]))
 
         silu = sb.tile([P, 4, NQ], F32, name="silu")
-        for pair in range(2):
-            scores = ps.tile([P, 2, NQ], F32, name="scores%d" % pair)
-            for u in range(2):
-                t = 2 * pair + u
-                nc.tensor.matmul_mx(
-                    scores[:, u, :],
-                    lhsT=k_codes[:, t * P : (t + 1) * P].bitcast(FP8X4),
-                    lhsT_scale=k_plane[:, t * P : (t + 1) * P],
-                    rhs=q_codes[:].bitcast(FP8X4),
-                    rhs_scale=q_plane[:],
-                    start=True,
-                    stop=True,
-                )
-            for u in range(2):
-                t = 2 * pair + u
-                nc.scalar.activation(silu[:, t, :], scores[:, u, :], ACT.Silu, bias=kb_cols[:, t : t + 1])
+        for t in range(4):
+            scores = ps.tile([P, NQ], F32, name="scores%d" % t, tag="scores%d" % t)
+            nc.tensor.matmul_mx(
+                scores[:],
+                lhsT=k_codes[:, t * P : (t + 1) * P].bitcast(FP8X4),
+                lhsT_scale=k_plane[:, t * P : (t + 1) * P],
+                rhs=q_codes[:].bitcast(FP8X4),
+                rhs_scale=q_plane[:],
+                start=True,
+                stop=True,
+            )
+            nc.scalar.activation(silu[:, t, :], scores[:], ACT.Silu, bias=kb_cols[:, t : t + 1])
 
-        def values(c):
-            got = sb.tile([P, N], BF16, name="v_got%d" % c, align_bytes=64)
+        vs_got = sb.tile([P, N], F32, name="vs_got", align_bytes=64)
+        vs_cols = token_columns(vs_pool, vs_got, "vs")
+
+        gate = sb.tile([P, 2, DV], F32, name="gate", tag="kb_gate")
+        nc.scalar.activation(gate[:], og_sb[:], ACT.Sigmoid)
+
+        v_bf = sb.tile([P, DV * 4], BF16, name="v_bf", tag="kb_og_v", align_bytes=64)
+        for c, (got_at, bank) in enumerate(((row_bytes, "kb_bank"), (row_bytes + 1024, "v_bank"))):
+            got = late.tile([P, N], BF16, name="v_got%d" % c, offset=got_at, align_bytes=64)
             nc.vector.tensor_copy(
                 got[:].rearrange("p (u g i c) -> p g u c i", u=2, i=4, c=2),
-                v_pool[:, c * T : (c + 1) * T].indirect(offsets[:]),
+                v_pool[c][:].indirect(offsets[:]),
             )
-            turned = ps.tile([P, 2, P], F32, name="v_turned%d" % c)
+            turned = ps.tile([P, 2, P], F32, name="v_turned%d" % c, tag=bank)
             words = got[:].bitcast(F32)
             for u in range(2):
                 nc.tensor.transpose(turned[:, u, :], words[:, u * P : (u + 1) * P], ident[:])
-            v_bf = sb.tile([P, P * 4], BF16, name="v_bf%d" % c, align_bytes=64)
             nc.scalar.copy(
-                v_bf[:].bitcast(F32).rearrange("p (e u) -> p e u", u=2),
+                v_bf[:].bitcast(F32)[:, c * 2 * P : (c + 1) * 2 * P].rearrange("p (e u) -> p e u", u=2),
                 turned[:].rearrange("p u e -> p e u"),
             )
-            return v_bf
 
-        w_bf = sb.tile([P, NQ, 4], BF16, name="w_bf", align_bytes=64)
-
-        def weights(h):
-            rows = slice(h * P, (h + 1) * P)
+        w_bf = []
+        for h in range(2):
+            w_half = late.tile([P, P, 4], BF16, name="w_bf%d" % h, offset=3 * row_bytes + 1024 * h, align_bytes=64)
             nc.vector.tensor_tensor(
-                w_bf[:, rows, :].rearrange("p (c i) t -> p c t i", i=2),
-                silu[:, :, rows].rearrange("p t (c i) -> p c t i", i=2),
-                vs_cols[:].unsqueeze(1).unsqueeze(3).to_broadcast([P, P // 2, 4, 2]),
+                w_half[:].rearrange("p (c i) t -> p c t i", i=2),
+                silu[:, :, h * P : (h + 1) * P].rearrange("p t (c i) -> p c t i", i=2),
+                vs_cols.unsqueeze(1).unsqueeze(3).to_broadcast([P, P // 2, 4, 2]),
                 MULT,
             )
+            w_bf.append(w_half)
 
-        v_bf0 = values(0)
-        weights(0)
-        v_bf1 = values(1)
-        weights(1)
-        w_codes = sb.tile([P, NQ], U32, name="w_codes", align_bytes=64)
-        w_plane = sb.tile([P, NQ], U8, name="w_plane", align_bytes=64)
-        nc.vector.quantize_mx(w_codes[:].bitcast(FP8X4), w_plane[:], w_bf[:].rearrange("p q t -> p (q t)"))
+        def quantised(name, grouped, width):
+            codes = sb.tile([P, width], U32, name=name + "_codes", align_bytes=64)
+            plane = sb.tile([P, width], U8, name=name + "_plane", align_bytes=64)
+            nc.vector.quantize_mx(codes[:].bitcast(FP8X4), plane[:], grouped)
+            return codes, plane
 
-        out_rows = out[0].rearrange("(h p) e -> p h e", p=P)
-        for c, v_bf in enumerate((v_bf0, v_bf1)):
-            v_codes = sb.tile([P, P], U32, name="v_codes%d" % c, align_bytes=64)
-            v_plane = sb.tile([P, P], U8, name="v_plane%d" % c, align_bytes=64)
-            nc.vector.quantize_mx(v_codes[:].bitcast(FP8X4), v_plane[:], v_bf[:])
-            y = ps.tile([P, 2, P], F32, name="y%d" % c)
-            for h in range(2):
-                nc.tensor.matmul_mx(
-                    y[:, h, :],
-                    lhsT=w_codes[:, h * P : (h + 1) * P].bitcast(FP8X4),
-                    lhsT_scale=w_plane[:, h * P : (h + 1) * P],
-                    rhs=v_codes[:].bitcast(FP8X4),
-                    rhs_scale=v_plane[:],
-                    start=True,
-                    stop=True,
-                )
-            result = sb.tile([P, 2, P], F32, name="result%d" % c)
-            nc.vector.scalar_tensor_tensor(
-                result[:], y[:], 1.0 / 16.0, gate[:, :, c * P : (c + 1) * P], MULT, MULT
+        w0 = quantised("w0", w_bf[0][:].rearrange("p q t -> p (q t)"), P)
+        w1 = quantised("w1", w_bf[1][:].rearrange("p q t -> p (q t)"), P)
+        v_codes, v_plane = quantised("v", v_bf[:], DV)
+
+        for h, (w_codes, w_plane) in enumerate((w0, w1)):
+            y = ps.tile([P, DV], F32, name="y%d" % h, tag=("y_bank", "scores0")[h])
+            nc.tensor.matmul_mx(
+                y[:],
+                lhsT=w_codes[:].bitcast(FP8X4),
+                lhsT_scale=w_plane[:],
+                rhs=v_codes[:].bitcast(FP8X4),
+                rhs_scale=v_plane[:],
+                start=True,
+                stop=True,
             )
-            nc.sync.dma_start(out_rows[:, :, c * P : (c + 1) * P], result[:])
+            result = sb.tile([P, DV], F32, name="result%d" % h)
+            nc.vector.scalar_tensor_tensor(result[:], y[:], 1.0 / 16.0, gate[:, h, :], MULT, MULT)
+            nc.sync.dma_start(out[0, h * P : (h + 1) * P, :], result[:])

@@ -29,9 +29,25 @@ def tile_attend_silu_gate_bias_srt_kernel(tc, qT, k_words, k_scales, vT, vs, kb,
 
         row_bytes = T * 4
         ks_pool = sb.tile([P, T], U8, name="ks_pool", align_bytes=64)
-        blank = late.tile([P, 2 * T + P], F32, name="blank", offset=row_bytes - 256, align_bytes=64)
+        kb_pool = late.tile([P, T], F32, name="kb_pool", offset=4 * row_bytes, align_bytes=64)
+        vs_pool = sb.tile([P, T], F32, name="vs_pool", align_bytes=64)
+        nc.vector.memset(ks_pool[:].bitcast(I32), 0)
+        nc.vector.memset(kb_pool[0 : P - 1, :], 0.0)
+        nc.vector.memset(vs_pool[0 : P - 1, :], 0.0)
+        nc.sync.dma_start(kb_pool[P - 1 : P, :], kb[0:1, :])
+        nc.sync.dma_start(vs_pool[P - 1 : P, :], vs[0:1, :])
+        kw_pool = late.tile([P, T], I32, name="kw_pool", offset=0, align_bytes=64)
+        nc.sync.dma_start(kw_pool[:], k_words[0].rearrange("p n t -> p (n t)").bitcast(I32))
+        q_raw = sb.tile([P, 4, NQ], F32, name="q_raw")
+        nc.sync.dma_start(q_raw[:], qT[0].rearrange("(p j) q -> p j q", j=4))
+        for quad in range(4):
+            nc.sync.dma_start(
+                ks_pool[32 * quad : 32 * quad + 4, :].bitcast(I32),
+                k_scales[0, 4 * quad : 4 * quad + 4, :].bitcast(I32),
+            )
+
+        blank = late.tile([P, 2 * T], F32, name="blank", offset=row_bytes + 2048, align_bytes=64)
         nc.gpsimd.memset(blank[:, 0:P], 0.0)
-        nc.gpsimd.memset(ks_pool[:].bitcast(I32), 0)
         ident = sb.tile([P, P], F32, name="ident")
         nc.gpsimd.affine_select(
             out=ident[:],
@@ -42,37 +58,22 @@ def tile_attend_silu_gate_bias_srt_kernel(tc, qT, k_words, k_scales, vT, vs, kb,
             pattern=[[-1, P]],
             channel_multiplier=1,
         )
-        warm = sb.tile([P, 1], F32, name="warm", tag="warm_q", align_bytes=64)
-        nc.scalar.activation(warm[:], ident[:, 0:1], ACT.Silu)
-
-        kb_pool = late.tile([P, T], F32, name="kb_pool", offset=4 * row_bytes, align_bytes=64)
-        nc.vector.memset(kb_pool[0 : P - 1, 0:767], 0.0)
-        nc.vector.memset(kb_pool[0 : P - 1, 767:1536], 0.0)
-        nc.gpsimd.memset(kb_pool[0 : P - 1, 1536:T], 0.0)
-        nc.sync.dma_start(kb_pool[P - 1 : P, :], kb[0:1, :])
-        q_raw = sb.tile([P, 4, NQ], F32, name="q_raw")
-        nc.sync.dma_start(q_raw[:], qT[0].rearrange("(p j) q -> p j q", j=4))
-        for quad in range(4):
-            nc.sync.dma_start(
-                ks_pool[32 * quad : 32 * quad + 4, :].bitcast(I32),
-                k_scales[0, 4 * quad : 4 * quad + 4, :].bitcast(I32),
-            )
-        kw_pool = late.tile([P, T], I32, name="kw_pool", offset=0, align_bytes=64)
-        nc.sync.dma_start(kw_pool[:], k_words[0].rearrange("p n t -> p (n t)").bitcast(I32))
-        vs_pool = late.tile([P, T], F32, name="vs_pool", offset=row_bytes, align_bytes=64)
-        nc.sync.dma_start(vs_pool[P - 1 : P, :], vs[0:1, :])
-        nc.gpsimd.memset(vs_pool[0 : P - 1, :], 0.0)
+        og_sb = late.tile([P, 2, DV], F32, name="og_sb", offset=row_bytes + 4096, align_bytes=64)
+        nc.sync.dma_start(og_sb[:], og[0].rearrange("(h p) e -> p h e", p=P))
         v_pool = []
         for c in range(2):
             v_half = late.tile([P, T], F32, name="v_pool%d" % c, offset=(2 + c) * row_bytes, align_bytes=64)
             nc.sync.dma_start(v_half[:], vT[c * P : (c + 1) * P, :])
             v_pool.append(v_half)
 
-        q_bf = sb.tile([P, NQ, 4], BF16, name="q_bf", tag="warm_q", align_bytes=64)
+        q_bf_at = 5 * row_bytes + 1024
+        q_bf = late.tile([P, NQ, 4], BF16, name="q_bf", offset=q_bf_at, align_bytes=64)
         nc.scalar.copy(
             q_bf[:].rearrange("p (c i) t -> p c t i", i=2),
             q_raw[:].rearrange("p t (c i) -> p c t i", i=2),
         )
+        gate = sb.tile([P, 2, DV], F32, name="gate")
+        nc.scalar.activation(gate[:], og_sb[:], ACT.Sigmoid)
 
         def dealt(tile):
             return tile[:].bitcast(U32).rearrange("p (t g i) -> p g t i", t=4, i=4)
@@ -84,24 +85,23 @@ def tile_attend_silu_gate_bias_srt_kernel(tc, qT, k_words, k_scales, vT, vs, kb,
                 nc.tensor.transpose(turned[:, t, :], got[:, t * P : (t + 1) * P], ident[:])
             return turned[:, :, P - 1]
 
-        kb_got = sb.tile([P, N], F32, name="kb_got", tag="kb_og_v", align_bytes=64)
-        kb_cols = sb.tile([P, 4], F32, name="kb_cols", tag="kb_gate")
+        kb_got = sb.tile([P, N], F32, name="kb_got", align_bytes=64)
+        kb_cols = sb.tile([P, 4], F32, name="kb_cols")
         nc.scalar.copy(kb_cols[:], token_columns(kb_pool, kb_got, "kb"))
-        og_sb = sb.tile([P, 2, DV], F32, name="og_sb", tag="kb_og_v", align_bytes=64)
-        nc.sync.dma_start(og_sb[:], og[0].rearrange("(h p) e -> p h e", p=P))
 
-        ks_got = late.tile([P, N], U8, name="ks_got", offset=4 * row_bytes, align_bytes=64)
+        k_codes = late.tile([P, N], U32, name="k_codes", offset=4 * row_bytes, align_bytes=64)
+        nc.vector.tensor_copy(dealt(k_codes), kw_pool[:].bitcast(U32).indirect(offsets[:]))
+        ks_got_at = 4 * row_bytes + 4096
+        ks_got = late.tile([P, N], U8, name="ks_got", offset=ks_got_at, align_bytes=64)
         nc.vector.tensor_copy(ks_got[:], ks_pool[:].indirect(offsets[:]))
         k_plane = sb.tile([P, N], U8, name="k_plane", align_bytes=64)
         nc.vector.tensor_copy(
             k_plane[:].bitcast(I32).rearrange("p (t g) -> p t g", t=4),
             ks_got[:].bitcast(I32).rearrange("p (g t) -> p t g", t=4),
         )
-        q_codes = late.tile([P, NQ], U32, name="q_codes", offset=4 * row_bytes + 1024, align_bytes=64)
+        q_codes = late.tile([P, NQ], U32, name="q_codes", offset=0, align_bytes=64)
         q_plane = sb.tile([P, NQ], U8, name="q_plane", align_bytes=64)
         nc.vector.quantize_mx(q_codes[:].bitcast(FP8X4), q_plane[:], q_bf[:].rearrange("p q t -> p (q t)"))
-        k_codes = late.tile([P, N], U32, name="k_codes", offset=4 * row_bytes + 2048, align_bytes=64)
-        nc.vector.tensor_copy(dealt(k_codes), kw_pool[:].bitcast(U32).indirect(offsets[:]))
 
         silu = sb.tile([P, 4, NQ], F32, name="silu")
         for t in range(4):
@@ -117,14 +117,11 @@ def tile_attend_silu_gate_bias_srt_kernel(tc, qT, k_words, k_scales, vT, vs, kb,
             )
             nc.scalar.activation(silu[:, t, :], scores[:], ACT.Silu, bias=kb_cols[:, t : t + 1])
 
-        vs_got = sb.tile([P, N], F32, name="vs_got", align_bytes=64)
+        vs_got = late.tile([P, N], F32, name="vs_got", offset=q_bf_at - 1024, align_bytes=64)
         vs_cols = token_columns(vs_pool, vs_got, "vs")
 
-        gate = sb.tile([P, 2, DV], F32, name="gate", tag="kb_gate")
-        nc.scalar.activation(gate[:], og_sb[:], ACT.Sigmoid)
-
-        v_bf = sb.tile([P, DV * 4], BF16, name="v_bf", tag="kb_og_v", align_bytes=64)
-        for c, (got_at, bank) in enumerate(((row_bytes, "kb_bank"), (row_bytes + 1024, "v_bank"))):
+        v_bf = sb.tile([P, DV * 4], BF16, name="v_bf", align_bytes=64)
+        for c, (got_at, bank) in enumerate(((ks_got_at - 768, "scores3"), (ks_got_at + 256, "v_bank"))):
             got = late.tile([P, N], BF16, name="v_got%d" % c, offset=got_at, align_bytes=64)
             nc.vector.tensor_copy(
                 got[:].rearrange("p (u g i c) -> p g u c i", u=2, i=4, c=2),

@@ -31,22 +31,23 @@ def tile_attend_silu_gate_bias_srt_kernel(tc, qT, k_words, k_scales, vT, vs, kb,
         ks_pool = sb.tile([P, T], U8, name="ks_pool", align_bytes=64)
         kb_pool = late.tile([P, T], F32, name="kb_pool", offset=4 * row_bytes, align_bytes=64)
         vs_pool = sb.tile([P, T], F32, name="vs_pool", align_bytes=64)
-        nc.vector.memset(ks_pool[:].bitcast(I32), 0)
-        nc.vector.memset(kb_pool[0 : P - 1, :], 0.0)
-        nc.vector.memset(vs_pool[0 : P - 1, :], 0.0)
+        nc.gpsimd.memset(ks_pool[:].bitcast(I32), 0)
+        nc.vector.memset(kb_pool[0 : P - 1, 0 : T // 2 - 1], 0.0)
+        nc.vector.memset(kb_pool[0 : P - 1, T // 2 - 1 : T], 0.0)
         nc.sync.dma_start(kb_pool[P - 1 : P, :], kb[0:1, :])
-        nc.sync.dma_start(vs_pool[P - 1 : P, :], vs[0:1, :])
+        vs_runs = sb.tile([P, T // P], F32, name="vs_runs")
+        nc.sync.dma_start(vs_runs[:], vs[0].rearrange("(p j) -> p j", p=P))
+        og_sb = sb.tile([P, 2, DV], F32, name="og_sb")
+        nc.sync.dma_start(og_sb[:], og[0].rearrange("(h p) e -> p h e", p=P))
         kw_pool = late.tile([P, T], I32, name="kw_pool", offset=0, align_bytes=64)
         nc.sync.dma_start(kw_pool[:], k_words[0].rearrange("p n t -> p (n t)").bitcast(I32))
-        q_raw = sb.tile([P, 4, NQ], F32, name="q_raw")
-        nc.sync.dma_start(q_raw[:], qT[0].rearrange("(p j) q -> p j q", j=4))
         for quad in range(4):
             nc.sync.dma_start(
                 ks_pool[32 * quad : 32 * quad + 4, :].bitcast(I32),
                 k_scales[0, 4 * quad : 4 * quad + 4, :].bitcast(I32),
             )
 
-        blank = late.tile([P, 2 * T], F32, name="blank", offset=row_bytes + 2048, align_bytes=64)
+        blank = late.tile([P, T + P], F32, name="blank", offset=2 * row_bytes - 256, align_bytes=64)
         nc.gpsimd.memset(blank[:, 0:P], 0.0)
         ident = sb.tile([P, P], F32, name="ident")
         nc.gpsimd.affine_select(
@@ -58,13 +59,24 @@ def tile_attend_silu_gate_bias_srt_kernel(tc, qT, k_words, k_scales, vT, vs, kb,
             pattern=[[-1, P]],
             channel_multiplier=1,
         )
-        og_sb = late.tile([P, 2, DV], F32, name="og_sb", offset=row_bytes + 4096, align_bytes=64)
-        nc.sync.dma_start(og_sb[:], og[0].rearrange("(h p) e -> p h e", p=P))
+        q_raw = late.tile([P, 4, NQ], F32, name="q_raw", offset=2 * row_bytes - 4096, align_bytes=64)
+        nc.sync.dma_start(q_raw[:], qT[0].rearrange("(p j) q -> p j q", j=4))
         v_pool = []
         for c in range(2):
             v_half = late.tile([P, T], F32, name="v_pool%d" % c, offset=(2 + c) * row_bytes, align_bytes=64)
             nc.sync.dma_start(v_half[:], vT[c * P : (c + 1) * P, :])
             v_pool.append(v_half)
+
+        gate = sb.tile([P, 2, DV], F32, name="gate")
+        nc.scalar.activation(gate[:], og_sb[:], ACT.Sigmoid)
+
+        vs_by_run = vs_pool[:].rearrange("p (n b j) -> p b n j", b=4, j=4)
+        for b in range(4):
+            spread = ps.tile([P, 4, P], F32, name="spread%d" % b, tag="scores%d" % b)
+            for j in range(4):
+                column = vs_runs[:, 4 * b + j : 4 * b + j + 1].to_broadcast([P, P])
+                nc.tensor.transpose(spread[:, j, :], column, ident[:])
+            nc.scalar.activation(vs_by_run[:, b], spread[:].rearrange("p j n -> p n j"), ACT.Copy)
 
         q_bf_at = 5 * row_bytes + 1024
         q_bf = late.tile([P, NQ, 4], BF16, name="q_bf", offset=q_bf_at, align_bytes=64)
@@ -72,8 +84,6 @@ def tile_attend_silu_gate_bias_srt_kernel(tc, qT, k_words, k_scales, vT, vs, kb,
             q_bf[:].rearrange("p (c i) t -> p c t i", i=2),
             q_raw[:].rearrange("p t (c i) -> p c t i", i=2),
         )
-        gate = sb.tile([P, 2, DV], F32, name="gate")
-        nc.scalar.activation(gate[:], og_sb[:], ACT.Sigmoid)
 
         def dealt(tile):
             return tile[:].bitcast(U32).rearrange("p (t g i) -> p g t i", t=4, i=4)

from contextlib import ExitStack

import concourse.mybir as mybir

F32 = mybir.dt.float32
BF16 = mybir.dt.bfloat16
I32 = mybir.dt.int32
U32 = mybir.dt.uint32
U16 = mybir.dt.uint16
U8 = mybir.dt.uint8
FP8X4 = mybir.dt.float8_e4m3fn_x4
ACT = mybir.ActivationFunctionType
MULT = mybir.AluOpType.mult

P = 128
T, N, D, DV, NQ = 2048, 512, 512, 256, 256
FLOPS = 2 * NQ * N * (D + DV)


def tile_attend_silu_gate_bias_srt_kernel(tc, qT, k_words, k_scales, vT, vs, kb, og, offs, out):
    nc = tc.nc
    with ExitStack() as ctx:
        sb = ctx.enter_context(tc.tile_pool(name="sb", bufs=1))
        late = ctx.enter_context(tc.tile_pool(name="late", bufs=1))
        ps = ctx.enter_context(tc.psum_pool(name="ps", bufs=1))

        offsets = sb.tile([P, N // 16], U16, name="offsets")
        nc.sync.dma_start(offsets[:], offs)

        row_bytes = T * 4
        ks_pool = sb.tile([P, T], U8, name="ks_pool", align_bytes=64)
        kb_pool = late.tile([P, T], F32, name="kb_pool", offset=4 * row_bytes, align_bytes=64)
        vs_pool = sb.tile([P, T], F32, name="vs_pool", align_bytes=64)
        nc.gpsimd.memset(ks_pool[:].bitcast(I32), 0)
        nc.vector.memset(kb_pool[0 : P - 1, 0 : T // 2 - 1], 0.0)
        nc.vector.memset(kb_pool[0 : P - 1, T // 2 - 1 : T], 0.0)
        nc.sync.dma_start(kb_pool[P - 1 : P, :], kb[0:1, :])
        vs_runs = sb.tile([P, T // P], F32, name="vs_runs")
        nc.sync.dma_start(vs_runs[:], vs[0].rearrange("(p j) -> p j", p=P))
        og_sb = sb.tile([P, 2, DV], F32, name="og_sb")
        nc.sync.dma_start(og_sb[:], og[0].rearrange("(h p) e -> p h e", p=P))
        kw_pool = late.tile([P, T], I32, name="kw_pool", offset=0, align_bytes=64)
        nc.sync.dma_start(kw_pool[:], k_words[0].rearrange("p n t -> p (n t)").bitcast(I32))
        for quad in range(4):
            nc.sync.dma_start(
                ks_pool[32 * quad : 32 * quad + 4, :].bitcast(I32),
                k_scales[0, 4 * quad : 4 * quad + 4, :].bitcast(I32),
            )

        blank = late.tile([P, T + P], F32, name="blank", offset=2 * row_bytes - 256, align_bytes=64)
        nc.gpsimd.memset(blank[:, 0:P], 0.0)
        ident = sb.tile([P, P], F32, name="ident")
        nc.gpsimd.affine_select(
            out=ident[:],
            in_=blank[:, 0:P],
            compare_op=mybir.AluOpType.not_equal,
            fill=1.0,
            base=0,
            pattern=[[-1, P]],
            channel_multiplier=1,
        )
        q_raw = late.tile([P, 4, NQ], F32, name="q_raw", offset=2 * row_bytes - 4096, align_bytes=64)
        nc.sync.dma_start(q_raw[:], qT[0].rearrange("(p j) q -> p j q", j=4))
        v_pool = []
        for c in range(2):
            v_half = late.tile([P, T], F32, name="v_pool%d" % c, offset=(2 + c) * row_bytes, align_bytes=64)
            nc.sync.dma_start(v_half[:], vT[c * P : (c + 1) * P, :])
            v_pool.append(v_half)

        gate = sb.tile([P, 2, DV], F32, name="gate")
        nc.scalar.activation(gate[:], og_sb[:], ACT.Sigmoid)

        vs_by_run = vs_pool[:].rearrange("p (n b j) -> p b n j", b=4, j=4)
        for b in range(4):
            spread = ps.tile([P, 4, P], F32, name="spread%d" % b, tag="scores%d" % b)
            for j in range(4):
                column = vs_runs[:, 4 * b + j : 4 * b + j + 1].to_broadcast([P, P])
                nc.tensor.transpose(spread[:, j, :], column, ident[:])
            nc.scalar.activation(vs_by_run[:, b], spread[:].rearrange("p j n -> p n j"), ACT.Copy)

        q_bf_at = 5 * row_bytes + 1024
        q_bf = late.tile([P, NQ, 4], BF16, name="q_bf", offset=q_bf_at, align_bytes=64)
        nc.scalar.copy(
            q_bf[:].rearrange("p (c i) t -> p c t i", i=2),
            q_raw[:].rearrange("p t (c i) -> p c t i", i=2),
        )

        def dealt(tile):
            return tile[:].bitcast(U32).rearrange("p (t g i) -> p g t i", t=4, i=4)

        def token_columns(pool, got, name):
            nc.vector.tensor_copy(dealt(got), pool[:].bitcast(U32).indirect(offsets[:]))
            turned = ps.tile([P, 4, P], F32, name=name + "_turned", tag=name + "_bank")
            for t in range(4):
                nc.tensor.transpose(turned[:, t, :], got[:, t * P : (t + 1) * P], ident[:])
            return turned[:, :, P - 1]

        kb_got = sb.tile([P, N], F32, name="kb_got", align_bytes=64)
        kb_cols = sb.tile([P, 4], F32, name="kb_cols")
        nc.scalar.copy(kb_cols[:], token_columns(kb_pool, kb_got, "kb"))

        k_codes = late.tile([P, N], U32, name="k_codes", offset=4 * row_bytes, align_bytes=64)
        nc.vector.tensor_copy(dealt(k_codes), kw_pool[:].bitcast(U32).indirect(offsets[:]))
        ks_got_at = 4 * row_bytes + 4096
        ks_got = late.tile([P, N], U8, name="ks_got", offset=ks_got_at, align_bytes=64)
        nc.vector.tensor_copy(ks_got[:], ks_pool[:].indirect(offsets[:]))
        k_plane = sb.tile([P, N], U8, name="k_plane", align_bytes=64)
        nc.vector.tensor_copy(
            k_plane[:].bitcast(I32).rearrange("p (t g) -> p t g", t=4),
            ks_got[:].bitcast(I32).rearrange("p (g t) -> p t g", t=4),
        )
        q_codes = late.tile([P, NQ], U32, name="q_codes", offset=0, align_bytes=64)
        q_plane = sb.tile([P, NQ], U8, name="q_plane", align_bytes=64)
        nc.vector.quantize_mx(q_codes[:].bitcast(FP8X4), q_plane[:], q_bf[:].rearrange("p q t -> p (q t)"))

        silu = sb.tile([P, 4, NQ], F32, name="silu")
        for t in range(4):
            scores = ps.tile([P, NQ], F32, name="scores%d" % t, tag="scores%d" % t)
            nc.tensor.matmul_mx(
                scores[:],
                lhsT=k_codes[:, t * P : (t + 1) * P].bitcast(FP8X4),
                lhsT_scale=k_plane[:, t * P : (t + 1) * P],
                rhs=q_codes[:].bitcast(FP8X4),
                rhs_scale=q_plane[:],
                start=True,
                stop=True,
            )
            nc.scalar.activation(silu[:, t, :], scores[:], ACT.Silu, bias=kb_cols[:, t : t + 1])

        vs_got = late.tile([P, N], F32, name="vs_got", offset=q_bf_at - 1024, align_bytes=64)
        vs_cols = token_columns(vs_pool, vs_got, "vs")

        v_bf = sb.tile([P, DV * 4], BF16, name="v_bf", align_bytes=64)
        for c, (got_at, bank) in enumerate(((ks_got_at - 768, "scores3"), (ks_got_at + 256, "v_bank"))):
            got = late.tile([P, N], BF16, name="v_got%d" % c, offset=got_at, align_bytes=64)
            nc.vector.tensor_copy(
                got[:].rearrange("p (u g i c) -> p g u c i", u=2, i=4, c=2),
                v_pool[c][:].indirect(offsets[:]),
            )
            turned = ps.tile([P, 2, P], F32, name="v_turned%d" % c, tag=bank)
            words = got[:].bitcast(F32)
            for u in range(2):
                nc.tensor.transpose(turned[:, u, :], words[:, u * P : (u + 1) * P], ident[:])
            nc.scalar.copy(
                v_bf[:].bitcast(F32)[:, c * 2 * P : (c + 1) * 2 * P].rearrange("p (e u) -> p e u", u=2),
                turned[:].rearrange("p u e -> p e u"),
            )

        w_bf = []
        for h in range(2):
            w_half = late.tile([P, P, 4], BF16, name="w_bf%d" % h, offset=3 * row_bytes + 1024 * h, align_bytes=64)
            nc.vector.tensor_tensor(
                w_half[:].rearrange("p (c i) t -> p c t i", i=2),
                silu[:, :, h * P : (h + 1) * P].rearrange("p t (c i) -> p c t i", i=2),
                vs_cols.unsqueeze(1).unsqueeze(3).to_broadcast([P, P // 2, 4, 2]),
                MULT,
            )
            w_bf.append(w_half)

        def quantised(name, grouped, width):
            codes = sb.tile([P, width], U32, name=name + "_codes", align_bytes=64)
            plane = sb.tile([P, width], U8, name=name + "_plane", align_bytes=64)
            nc.vector.quantize_mx(codes[:].bitcast(FP8X4), plane[:], grouped)
            return codes, plane

        w0 = quantised("w0", w_bf[0][:].rearrange("p q t -> p (q t)"), P)
        w1 = quantised("w1", w_bf[1][:].rearrange("p q t -> p (q t)"), P)
        v_codes, v_plane = quantised("v", v_bf[:], DV)

        for h, (w_codes, w_plane) in enumerate((w0, w1)):
            y = ps.tile([P, DV], F32, name="y%d" % h, tag=("y_bank", "scores0")[h])
            nc.tensor.matmul_mx(
                y[:],
                lhsT=w_codes[:].bitcast(FP8X4),
                lhsT_scale=w_plane[:],
                rhs=v_codes[:].bitcast(FP8X4),
                rhs_scale=v_plane[:],
                start=True,
                stop=True,
            )
            result = sb.tile([P, DV], F32, name="result%d" % h)
            nc.vector.scalar_tensor_tensor(result[:], y[:], 1.0 / 16.0, gate[:, h, :], MULT, MULT)
            nc.sync.dma_start(out[0, h * P : (h + 1) * P, :], result[:])
